import numpy as np
import ml_dtypes


def mxq(x, axis, fmt="e4m3"):
    dtype, down = {"e4m3": (ml_dtypes.float8_e4m3fn, 7), "e5m2": (ml_dtypes.float8_e5m2, 14)}[fmt]
    v = np.moveaxis(np.asarray(x, np.float32).astype(ml_dtypes.bfloat16).astype(np.float64), axis, -1)
    blocks = v.reshape(v.shape[:-1] + (-1, 32))
    amax = np.abs(blocks).max(-1, keepdims=True)
    byte = np.maximum(np.where(amax > 0, np.frexp(amax)[1] - 1 + 127, 0) - down, 1)
    scale = np.exp2(byte - 127.0)
    codes = (blocks / scale).astype(np.float32).astype(dtype).astype(np.float64)
    return np.moveaxis((codes * scale).reshape(v.shape), -1, axis)


WIDE = False


def mx_kscale(k):
    if not WIDE:
        return np.ones(k)
    levels = np.array([30, -30])
    if k % 512:
        return np.exp2(np.random.permutation(np.resize(levels, k // 32))).repeat(32)
    a = np.empty((k // 512, 16))
    for p in range(k // 512):
        a[p, :8] = np.random.permutation(np.resize(levels, 8))
        for g in range(8):
            far = levels[np.abs(levels - a[p, g]) >= 10]
            a[p, g + 8] = far[np.random.randint(len(far))]
    return np.exp2(a.ravel()).repeat(32)


BF16 = ml_dtypes.bfloat16


def bf(x):
    return np.asarray(x, np.float32).astype(BF16)


def f64(x):
    return np.asarray(x).astype(np.float64)


E2M1 = np.array([0.0, 0.5, 1.0, 1.5, 2.0, 3.0, 4.0, 6.0, -0.0, -0.5, -1.0, -1.5, -2.0, -3.0, -4.0, -6.0])


def pack_weight(w, fmt):
    k, n = w.shape
    w = f64(bf(w)).reshape(k // 32, 32, n)
    amax = np.abs(w).max(1)
    if fmt == "e4m3":
        byte = np.frexp(amax)[1] - 1 + 127 - 7
    else:
        mant, ex = np.frexp(amax / 6.0)
        byte = np.where(mant > 0.5, ex, ex - 1) + 127
    byte = np.clip(np.where(amax > 0, byte, 1), 1, 254)
    scaled = (w * np.exp2(127.0 - byte)[:, None, :]).reshape(k, n).astype(np.float32)
    by_word = np.ascontiguousarray(scaled.reshape(k // 512, 128, 4, n).transpose(0, 1, 3, 2))
    if fmt == "e4m3":
        words = by_word.astype(ml_dtypes.float8_e4m3fn).view(np.uint8)
    else:
        c = by_word.astype(ml_dtypes.float4_e2m1fn).view(np.uint8) & 0xF
        words = c[..., 0::2] | (c[..., 1::2] << 4)
    return np.ascontiguousarray(words), np.ascontiguousarray(byte.astype(np.uint8).reshape(k // 512, 16, n))


def unpack_weight(words, scales, fmt):
    g, p, n, _ = words.shape
    if fmt == "e4m3":
        vals = np.ascontiguousarray(words).view(ml_dtypes.float8_e4m3fn).astype(np.float64)
    else:
        nib = np.empty((g, p, n, 4), np.uint8)
        nib[..., 0::2] = words & 0xF
        nib[..., 1::2] = words >> 4
        vals = E2M1[nib]
    vals = vals * np.repeat(np.exp2(scales.astype(np.float64) - 127.0), 8, axis=1)[..., None]
    return vals.transpose(0, 1, 3, 2).reshape(g * 512, n)
def pack4(w):
    words, scales = pack_weight(w, "e2m1")
    return words.reshape(words.shape[0], 128, -1), scales


def unpack4(words, scales):
    return unpack_weight(words.reshape(words.shape[0], 128, -1, 2), scales, "e2m1")


M, K, N, D = 1024, 1024, 2048, 512


def setup_inputs():
    s = mx_kscale(K)
    t = mx_kscale(N)
    left = np.random.standard_normal((M, K)) * s
    right = np.random.standard_normal((K, N)) / np.sqrt(K) / s[:, None]
    right_words, right_scales = pack4(right)
    vis = np.random.uniform(0.5, 1.5, N) * t
    codes = np.random.standard_normal((N, D)) / np.sqrt(N) / t[:, None]
    return {"left": bf(left),
            "right_words": right_words,
            "right_scales": right_scales,
            "vis": bf(vis),
            "codes": bf(codes)}


def reference(left, right_words, right_scales, vis, codes):
    corr = mxq(f64(left), 1, "e4m3") @ unpack4(right_words, right_scales)
    e = np.exp(corr)
    mass = e.mean(axis=1, keepdims=True)
    w = e * f64(vis)
    num = mxq(w, 1, "e5m2") @ mxq(f64(codes), 0, "e4m3")
    return num / mass

@@ -1,0 +1,277 @@
+from contextlib import ExitStack
+
+import concourse.mybir as mybir
+from concourse.masks import make_identity
+
+M, K, N, D = 1024, 1024, 2048, 512
+FLOPS = 2 * M * K * N + 2 * M * N * D
+
+F32 = mybir.dt.float32
+BF16 = mybir.dt.bfloat16
+I32 = mybir.dt.int32
+U32 = mybir.dt.uint32
+U8 = mybir.dt.uint8
+E4M3X4 = mybir.dt.float8_e4m3fn_x4
+E5M2X4 = mybir.dt.float8_e5m2_x4
+E2M1X4 = mybir.dt.float4_e2m1fn_x4
+ACT = mybir.ActivationFunctionType
+ALU = mybir.AluOpType
+
+P = 128
+PASS = 512
+TILES = M // P
+K_PASSES = K // PASS
+GROUPS = N // PASS
+HALVES = GROUPS // 2
+MIX_LAG = 4
+RUN_AHEAD = 2
+
+
+def tile_stereo_softmax_code_mix_s9_kernel(tc, left, right_words, right_scales, vis, codes, out):
+    nc = tc.nc
+    with ExitStack() as ctx:
+        keep = ctx.enter_context(tc.tile_pool(name="keep", bufs=1))
+        work = ctx.enter_context(tc.tile_pool(name="work", bufs=4))
+        psum = ctx.enter_context(tc.psum_pool(name="psum", bufs=1))
+        ctx.enter_context(tc.manual_schedule())
+
+        def acc_bank(name):
+            return psum.tile([P, PASS], F32, tag="acc", bufs=5, name=name)
+
+        def turn_bank(name):
+            return psum.tile([P, 4, P], F32, tag="turn", bufs=3, name=name)
+
+        r_scales = keep.tile([P, K_PASSES, N], U8, align_bytes=64)
+        zeros = keep.tile([P, P], BF16)
+        vis_row = keep.tile([P, N], BF16)
+        nc.vector.memset(zeros[:], 0.0)
+        nc.vector.memset(vis_row[:].bitcast(I32), 0)
+        nc.vector.memset(r_scales[:].bitcast(I32), 0)
+        ident = keep.tile([P, P], F32)
+        make_identity(nc, ident[:])
+        ones = keep.tile([P, P], BF16)
+        nc.scalar.activation(out=ones[:], in_=zeros[:], func=ACT.Exp)
+
+        left_raw = [keep.tile([P, K], BF16, name="left_raw%d" % i) for i in range(TILES)]
+        r_words = [keep.tile([P, K_PASSES, 2 * PASS], U8, align_bytes=64, name="r_words%d" % g) for g in range(GROUPS)]
+        codes_raw = [keep.tile([P, 4, D], BF16, name="codes_raw%d" % g) for g in range(GROUPS)]
+
+        def load_left(i):
+            nc.sync.dma_start(out=left_raw[i][:], in_=left[i * P:(i + 1) * P, :])
+
+        def load_right(g):
+            src = right_words[:, :, 2 * PASS * g:2 * PASS * (g + 1)].rearrange("c p n -> p c n")
+            nc.sync.dma_start(out=r_words[g][:].bitcast(I32), in_=src.bitcast(I32))
+
+        def load_codes(g):
+            src = codes[g * PASS:(g + 1) * PASS, :].rearrange("(p t) d -> p t d", t=4)
+            nc.sync.dma_start(out=codes_raw[g][:], in_=src)
+
+        load_left(0)
+        load_right(0)
+        nc.sync.dma_start(out=vis_row[0:1, :], in_=vis.rearrange("(o n) -> o n", o=1))
+        for r in range(4):
+            src = right_scales[:, 4 * r:4 * r + 4, :].rearrange("c q n -> q c n")
+            nc.sync.dma_start(out=r_scales[32 * r:32 * r + 4, :, :].bitcast(I32), in_=src.bitcast(I32))
+        load_codes(0)
+        load_right(1)
+        load_left(1)
+        load_right(2)
+        load_right(3)
+        for g in range(1, GROUPS):
+            load_left(g + 1)
+            load_codes(g)
+        for i in range(GROUPS + 1, TILES):
+            load_left(i)
+
+        banks, turned, left_q, e_tiles, w_tiles, w_q, codes_il, codes_q = {}, {}, {}, {}, {}, {}, {}, {}
+        mixes = {}
+        sums = keep.tile([P, TILES, GROUPS], F32, name="sums")
+        totals = keep.tile([P, TILES], F32, name="totals")
+        means = keep.tile([P, TILES], F32, name="means")
+        inv_mass = keep.tile([P, TILES], F32, name="inv_mass")
+        vis_all = keep.tile([P, N], BF16)
+
+        def turn_left(i):
+            bank = turn_bank("left_bank")
+            words = left_raw[i][:].bitcast(F32)
+            for c in range(K_PASSES):
+                for u in range(2):
+                    nc.tensor.transpose(bank[:, 2 * c + u, :], words[:, 256 * c + u:256 * (c + 1):2], ident[:])
+            banks["left", i] = bank
+
+        def turn_w(i, h, spare=False):
+            if spare:
+                bank = psum.tile([P, 4, P], F32, tag="acc", bufs=5, name="w_bank")
+            else:
+                bank = turn_bank("w_bank")
+            words = w_tiles[i, h][:].bitcast(F32)
+            for s in range(4):
+                nc.tensor.transpose(bank[:, s, :], words[:, P * s:P * (s + 1)], ident[:])
+            banks["w", i, h] = bank
+
+        def copy_turned(key, on_scalar):
+            dst = work.tile([P, 2 * PASS], BF16, tag="turned", bufs=8, align_bytes=64, name="turned")
+            src = banks[key][:].rearrange("p (c u) m -> p c m u", u=2)
+            dst_words = dst[:].bitcast(F32).rearrange("p (c m u) -> p c m u", c=2, u=2)
+            if on_scalar:
+                nc.scalar.copy(out=dst_words, in_=src)
+            else:
+                nc.vector.tensor_copy(out=dst_words, in_=src)
+            turned[key] = dst
+
+        def quantise(src, fmt, tag, bufs):
+            width = src.shape[1] // 4
+            words = work.tile([P, width], U32, tag=tag + "_words", bufs=bufs, align_bytes=64, name=tag + "_words")
+            scales = work.tile([P, width], U8, tag=tag + "_scales", bufs=bufs, align_bytes=64, name=tag + "_scales")
+            nc.vector.quantize_mx(out=words[:].bitcast(fmt), scales=scales[:], in_=src)
+            return words, scales
+
+        def quantise_left(i):
+            left_q[i] = quantise(turned["left", i][:], E4M3X4, "left", 3)
+
+        def quantise_w(i, h):
+            w_q[i, h] = quantise(turned["w", i, h][:], E5M2X4, "w", 12)
+
+        def interleave_codes(g):
+            dst = work.tile([P, D, 4], BF16, tag="codes_il", bufs=2, align_bytes=64, name="codes_il")
+            nc.vector.tensor_copy(out=dst[:], in_=codes_raw[g][:].rearrange("p t d -> p d t"))
+            codes_il[g] = dst
+
+        def quantise_codes(g):
+            codes_q[g] = quantise(codes_il[g][:].rearrange("p d t -> p (d t)"), E4M3X4, "codes", GROUPS)
+
+        def spread_vis(h):
+            bank = psum.tile([P, 2 * PASS], BF16, tag="turn", bufs=3, name="vis_bank")
+            for c in range(2):
+                g = 2 * h + c
+                nc.tensor.matmul(bank[:, c * PASS:(c + 1) * PASS], lhsT=ones[:], rhs=vis_row[:, g * PASS:(g + 1) * PASS],
+                                 start=True, stop=True)
+            dst = vis_all[:, 2 * PASS * h:2 * PASS * (h + 1)].rearrange("q (c u p e) -> q c u p e", c=2, u=2, e=2)
+            nc.scalar.copy(out=dst, in_=bank[:].rearrange("q (c p u e) -> q c u p e", c=2, u=2, e=2))
+
+        def correlate(i, g):
+            words, scales = left_q[i]
+            bank = acc_bank("corr")
+            for c in range(K_PASSES):
+                nc.tensor.matmul_mx(
+                    out=bank[:],
+                    lhsT=words[:, c * P:(c + 1) * P].bitcast(E4M3X4),
+                    lhsT_scale=scales[:, c * P:(c + 1) * P],
+                    rhs=r_words[g][:, c, :].bitcast(E2M1X4),
+                    rhs_scale=r_scales[:, c, g * PASS:(g + 1) * PASS],
+                    start=(c == 0), stop=(c == K_PASSES - 1))
+            h, c = divmod(g, 2)
+            if c == 0:
+                e_tiles[i, h] = work.tile([P, 2 * PASS], F32, tag="e", bufs=10, name="e")
+            dst = e_tiles[i, h][:, c * PASS:(c + 1) * PASS].rearrange("m (u p e) -> m u p e", u=2, e=2)
+            nc.scalar.activation(out=dst, in_=bank[:].rearrange("m (p u e) -> m u p e", u=2, e=2), func=ACT.Exp,
+                                 accum_out=sums[:, i, g:g + 1])
+
+        def weigh(i, h):
+            w = work.tile([P, 2 * PASS], BF16, tag="w", bufs=8, name="w")
+            nc.vector.tensor_tensor(out=w[:], in0=e_tiles[i, h][:],
+                                    in1=vis_all[:, 2 * PASS * h:2 * PASS * (h + 1)], op=ALU.mult)
+            w_tiles[i, h] = w
+
+        def add_up(lo, hi):
+            nc.vector.tensor_reduce(out=totals[:, lo:hi], in_=sums[:, lo:hi, :], axis=mybir.AxisListType.X, op=ALU.add)
+
+        def average(lo, hi):
+            nc.vector.tensor_scalar(out=means[:, lo:hi], in0=totals[:, lo:hi], scalar1=1.0 / N, scalar2=None, op0=ALU.mult)
+
+        def invert(lo, hi):
+            nc.vector.reciprocal(out=inv_mass[:, lo:hi], in_=means[:, lo:hi])
+
+        def mix(i):
+            bank = acc_bank("mix")
+            for g in range(GROUPS):
+                h, c = divmod(g, 2)
+                words, scales = w_q[i, h]
+                c_words, c_scales = codes_q[g]
+                nc.tensor.matmul_mx(
+                    out=bank[:],
+                    lhsT=words[:, c * P:(c + 1) * P].bitcast(E5M2X4),
+                    lhsT_scale=scales[:, c * P:(c + 1) * P],
+                    rhs=c_words[:].bitcast(E4M3X4),
+                    rhs_scale=c_scales[:],
+                    start=(g == 0), stop=(g == GROUPS - 1))
+            mixes[i] = bank
+
+        def finish(i):
+            result = work.tile([P, D], F32, tag="result", name="result")
+            nc.scalar.activation(out=result[:], in_=mixes[i][:], func=ACT.Copy, scale=inv_mass[:, i:i + 1])
+            nc.sync.dma_start(out=out[i * P:(i + 1) * P, :], in_=result[:])
+
+        turn_left(0)
+        copy_turned(("left", 0), True)
+        quantise_left(0)
+        for h in range(HALVES):
+            spread_vis(h)
+
+        last = TILES - 1
+        halves = [(i, h) for i in range(TILES) for h in range(HALVES)]
+        turned_n = quantised = 0
+        for i in range(TILES):
+            if 1 <= i < last:
+                quantise_left(i + 1)
+            to_quantise = halves[quantised:turned_n]
+            quantised = turned_n
+            batch = (i - 3, i) if i > 0 and i % 3 == 0 else None
+            if batch:
+                add_up(*batch)
+            for half in to_quantise[:1]:
+                quantise_w(*half)
+            if batch:
+                average(*batch)
+            for half in to_quantise[1:]:
+                quantise_w(*half)
+            if batch:
+                invert(*batch)
+            correlate(i, 0)
+            correlate(i, 1)
+            if i == 0:
+                turn_left(1)
+                copy_turned(("left", 1), True)
+            if i == 0:
+                interleave_codes(0)
+                quantise_codes(0)
+                quantise_left(1)
+                weigh(*halves[0])
+            elif i < GROUPS:
+                interleave_codes(i)
+                weigh(*halves[i])
+                quantise_codes(i)
+            correlate(i, 2)
+            correlate(i, 3)
+            if i >= GROUPS:
+                for half in halves[3 * i - 8:3 * i - 5]:
+                    weigh(*half)
+            if i >= MIX_LAG:
+                mix(i - MIX_LAG)
+                finish(i - MIX_LAG)
+            free_banks = 3
+            if i + 2 < TILES:
+                turn_left(i + 2)
+                copy_turned(("left", i + 2), True)
+                free_banks = 2
+            if i >= 3:
+                for n, half in enumerate(halves[turned_n:turned_n + free_banks]):
+                    turn_w(*half)
+                    copy_turned(("w",) + half, n < 2)
+                turned_n = turned_n + free_banks
+
+        rest = (last // 3 * 3, TILES)
+        add_up(*rest)
+        for n, half in enumerate(halves[turned_n:]):
+            turn_w(*half, True)
+            copy_turned(("w",) + half, True)
+        for n, half in enumerate(halves[quantised:]):
+            quantise_w(*half)
+            if n == 0:
+                average(*rest)
+            if n == 1:
+                invert(*rest)
+        for i in range(TILES - MIX_LAG, TILES):
+            mix(i)
+            finish(i)

@@ -24,7 +24,7 @@ K_PASSES = K // PASS
 GROUPS = N // PASS
 HALVES = GROUPS // 2
 MIX_LAG = 4
-RUN_AHEAD = 2
+TURN_START = 3
 
 
 def tile_stereo_softmax_code_mix_s9_kernel(tc, left, right_words, right_scales, vis, codes, out):
@@ -41,19 +41,19 @@ def tile_stereo_softmax_code_mix_s9_kernel(tc, left, right_words, right_scales, 
         def turn_bank(name):
             return psum.tile([P, 4, P], F32, tag="turn", bufs=3, name=name)
 
-        r_scales = keep.tile([P, K_PASSES, N], U8, align_bytes=64)
+        r_scales = keep.tile([P, K_PASSES, N], U8, align_bytes=256)
         zeros = keep.tile([P, P], BF16)
         vis_row = keep.tile([P, N], BF16)
+        nc.vector.memset(r_scales[:].bitcast(I32), 0)
         nc.vector.memset(zeros[:], 0.0)
         nc.vector.memset(vis_row[:].bitcast(I32), 0)
-        nc.vector.memset(r_scales[:].bitcast(I32), 0)
         ident = keep.tile([P, P], F32)
         make_identity(nc, ident[:])
         ones = keep.tile([P, P], BF16)
         nc.scalar.activation(out=ones[:], in_=zeros[:], func=ACT.Exp)
 
         left_raw = [keep.tile([P, K], BF16, name="left_raw%d" % i) for i in range(TILES)]
-        r_words = [keep.tile([P, K_PASSES, 2 * PASS], U8, align_bytes=64, name="r_words%d" % g) for g in range(GROUPS)]
+        r_words = [keep.tile([P, K_PASSES, 2 * PASS], U8, align_bytes=256, name="r_words%d" % g) for g in range(GROUPS)]
         codes_raw = [keep.tile([P, 4, D], BF16, name="codes_raw%d" % g) for g in range(GROUPS)]
 
         def load_left(i):
@@ -68,11 +68,11 @@ def tile_stereo_softmax_code_mix_s9_kernel(tc, left, right_words, right_scales, 
             nc.sync.dma_start(out=codes_raw[g][:], in_=src)
 
         load_left(0)
-        load_right(0)
-        nc.sync.dma_start(out=vis_row[0:1, :], in_=vis.rearrange("(o n) -> o n", o=1))
         for r in range(4):
             src = right_scales[:, 4 * r:4 * r + 4, :].rearrange("c q n -> q c n")
             nc.sync.dma_start(out=r_scales[32 * r:32 * r + 4, :, :].bitcast(I32), in_=src.bitcast(I32))
+        nc.sync.dma_start(out=vis_row[0:1, :], in_=vis.rearrange("(o n) -> o n", o=1))
+        load_right(0)
         load_codes(0)
         load_right(1)
         load_left(1)
@@ -111,7 +111,7 @@ def tile_stereo_softmax_code_mix_s9_kernel(tc, left, right_words, right_scales, 
             banks["w", i, h] = bank
 
         def copy_turned(key, on_scalar):
-            dst = work.tile([P, 2 * PASS], BF16, tag="turned", bufs=8, align_bytes=64, name="turned")
+            dst = work.tile([P, 2 * PASS], BF16, tag="turned", bufs=8, align_bytes=256, name="turned")
             src = banks[key][:].rearrange("p (c u) m -> p c m u", u=2)
             dst_words = dst[:].bitcast(F32).rearrange("p (c m u) -> p c m u", c=2, u=2)
             if on_scalar:
@@ -122,8 +122,8 @@ def tile_stereo_softmax_code_mix_s9_kernel(tc, left, right_words, right_scales, 
 
         def quantise(src, fmt, tag, bufs):
             width = src.shape[1] // 4
-            words = work.tile([P, width], U32, tag=tag + "_words", bufs=bufs, align_bytes=64, name=tag + "_words")
-            scales = work.tile([P, width], U8, tag=tag + "_scales", bufs=bufs, align_bytes=64, name=tag + "_scales")
+            words = work.tile([P, width], U32, tag=tag + "_words", bufs=bufs, align_bytes=256, name=tag + "_words")
+            scales = work.tile([P, width], U8, tag=tag + "_scales", bufs=bufs, align_bytes=256, name=tag + "_scales")
             nc.vector.quantize_mx(out=words[:].bitcast(fmt), scales=scales[:], in_=src)
             return words, scales
 
@@ -134,8 +134,9 @@ def tile_stereo_softmax_code_mix_s9_kernel(tc, left, right_words, right_scales, 
             w_q[i, h] = quantise(turned["w", i, h][:], E5M2X4, "w", 12)
 
         def interleave_codes(g):
-            dst = work.tile([P, D, 4], BF16, tag="codes_il", bufs=2, align_bytes=64, name="codes_il")
-            nc.vector.tensor_copy(out=dst[:], in_=codes_raw[g][:].rearrange("p t d -> p d t"))
+            dst = work.tile([P, D, 4], BF16, tag="codes_il", bufs=2, align_bytes=256, name="codes_il")
+            nc.vector.tensor_copy(out=dst[:].rearrange("p (c i) t -> p c t i", i=4),
+                                  in_=codes_raw[g][:].rearrange("p t (c i) -> p c t i", i=4))
             codes_il[g] = dst
 
         def quantise_codes(g):
@@ -250,28 +251,31 @@ def tile_stereo_softmax_code_mix_s9_kernel(tc, left, right_words, right_scales, 
             if i >= MIX_LAG:
                 mix(i - MIX_LAG)
                 finish(i - MIX_LAG)
-            free_banks = 3
             if i + 2 < TILES:
                 turn_left(i + 2)
                 copy_turned(("left", i + 2), True)
-                free_banks = 2
-            if i >= 3:
-                for n, half in enumerate(halves[turned_n:turned_n + free_banks]):
-                    turn_w(*half)
-                    copy_turned(("w",) + half, n < 2)
-                turned_n = turned_n + free_banks
+            if i >= TURN_START:
+                count = 2 if i + 2 < TILES else 4
+                for n, half in enumerate(halves[turned_n:turned_n + count]):
+                    turn_w(*half, n == 3)
+                    copy_turned(("w",) + half, n != 0 or i < 6)
+                turned_n = turned_n + count
 
         rest = (last // 3 * 3, TILES)
         add_up(*rest)
-        for n, half in enumerate(halves[turned_n:]):
-            turn_w(*half, True)
-            copy_turned(("w",) + half, True)
-        for n, half in enumerate(halves[quantised:]):
+        for n, half in enumerate(halves[quantised:turned_n]):
             quantise_w(*half)
             if n == 0:
                 average(*rest)
             if n == 1:
                 invert(*rest)
-        for i in range(TILES - MIX_LAG, TILES):
+        mix(TILES - MIX_LAG)
+        finish(TILES - MIX_LAG)
+        for n, half in enumerate(halves[turned_n:]):
+            turn_w(*half)
+            copy_turned(("w",) + half, n != 1)
+        for half in halves[turned_n:]:
+            quantise_w(*half)
+        for i in range(TILES - MIX_LAG + 1, TILES):
             mix(i)
             finish(i)

@@ -35,22 +35,25 @@ def tile_stereo_softmax_code_mix_s9_kernel(tc, left, right_words, right_scales, 
         psum = ctx.enter_context(tc.psum_pool(name="psum", bufs=1))
         ctx.enter_context(tc.manual_schedule())
 
-        def acc_bank(name):
-            return psum.tile([P, PASS], F32, tag="acc", bufs=5, name=name)
+        handed_out = []
 
-        def turn_bank(name):
-            return psum.tile([P, 4, P], F32, tag="turn", bufs=3, name=name)
+        def next_bank(shape, dtype, name):
+            handed_out.append(name)
+            return psum.tile(shape, dtype, tag="bank%d" % (len(handed_out) % 8), name=name)
 
         r_scales = keep.tile([P, K_PASSES, N], U8, align_bytes=256)
-        zeros = keep.tile([P, P], BF16)
+        zeros = keep.tile([P, PASS], BF16)
         vis_row = keep.tile([P, N], BF16)
+        nc.vector.memset(zeros[:].bitcast(I32), 0)
         nc.vector.memset(r_scales[:].bitcast(I32), 0)
-        nc.vector.memset(zeros[:], 0.0)
         nc.vector.memset(vis_row[:].bitcast(I32), 0)
         ident = keep.tile([P, P], F32)
         make_identity(nc, ident[:])
         ones = keep.tile([P, P], BF16)
-        nc.scalar.activation(out=ones[:], in_=zeros[:], func=ACT.Exp)
+        nc.scalar.activation(out=ones[:], in_=zeros[:, :P], func=ACT.Exp)
+        warm = next_bank([P, PASS], F32, "warm")
+        for n in range(4):
+            nc.tensor.matmul(warm[:], lhsT=zeros[:, :P], rhs=zeros[:], start=True, stop=True)
 
         left_raw = [keep.tile([P, K], BF16, name="left_raw%d" % i) for i in range(TILES)]
         r_words = [keep.tile([P, K_PASSES, 2 * PASS], U8, align_bytes=256, name="r_words%d" % g) for g in range(GROUPS)]
@@ -73,8 +76,8 @@ def tile_stereo_softmax_code_mix_s9_kernel(tc, left, right_words, right_scales, 
             nc.sync.dma_start(out=r_scales[32 * r:32 * r + 4, :, :].bitcast(I32), in_=src.bitcast(I32))
         nc.sync.dma_start(out=vis_row[0:1, :], in_=vis.rearrange("(o n) -> o n", o=1))
         load_right(0)
-        load_codes(0)
         load_right(1)
+        load_codes(0)
         load_left(1)
         load_right(2)
         load_right(3)
@@ -85,26 +88,33 @@ def tile_stereo_softmax_code_mix_s9_kernel(tc, left, right_words, right_scales, 
             load_left(i)
 
         banks, turned, left_q, e_tiles, w_tiles, w_q, codes_il, codes_q = {}, {}, {}, {}, {}, {}, {}, {}
-        mixes = {}
+        mixes, left_sorted = {}, {}
         sums = keep.tile([P, TILES, GROUPS], F32, name="sums")
         totals = keep.tile([P, TILES], F32, name="totals")
         means = keep.tile([P, TILES], F32, name="means")
         inv_mass = keep.tile([P, TILES], F32, name="inv_mass")
         vis_all = keep.tile([P, N], BF16)
 
+        def sort_left(i):
+            dst = work.tile([P, K_PASSES, 2, P], F32, tag="left_sorted", bufs=3, name="left_sorted")
+            src = left_raw[i][:].bitcast(F32).rearrange("m (c p u) -> m c u p", c=K_PASSES, u=2)
+            nc.vector.tensor_copy(out=dst[:], in_=src)
+            left_sorted[i] = dst
+
         def turn_left(i):
-            bank = turn_bank("left_bank")
+            bank = next_bank([P, 4, P], F32, "left_bank")
             words = left_raw[i][:].bitcast(F32)
             for c in range(K_PASSES):
                 for u in range(2):
-                    nc.tensor.transpose(bank[:, 2 * c + u, :], words[:, 256 * c + u:256 * (c + 1):2], ident[:])
+                    if i in left_sorted:
+                        src = left_sorted[i][:, c, u, :]
+                    else:
+                        src = words[:, 256 * c + u:256 * (c + 1):2]
+                    nc.tensor.transpose(bank[:, 2 * c + u, :], src, ident[:])
             banks["left", i] = bank
 
-        def turn_w(i, h, spare=False):
-            if spare:
-                bank = psum.tile([P, 4, P], F32, tag="acc", bufs=5, name="w_bank")
-            else:
-                bank = turn_bank("w_bank")
+        def turn_w(i, h):
+            bank = next_bank([P, 4, P], F32, "w_bank")
             words = w_tiles[i, h][:].bitcast(F32)
             for s in range(4):
                 nc.tensor.transpose(bank[:, s, :], words[:, P * s:P * (s + 1)], ident[:])
@@ -143,7 +153,7 @@ def tile_stereo_softmax_code_mix_s9_kernel(tc, left, right_words, right_scales, 
             codes_q[g] = quantise(codes_il[g][:].rearrange("p d t -> p (d t)"), E4M3X4, "codes", GROUPS)
 
         def spread_vis(h):
-            bank = psum.tile([P, 2 * PASS], BF16, tag="turn", bufs=3, name="vis_bank")
+            bank = next_bank([P, 2 * PASS], BF16, "vis_bank")
             for c in range(2):
                 g = 2 * h + c
                 nc.tensor.matmul(bank[:, c * PASS:(c + 1) * PASS], lhsT=ones[:], rhs=vis_row[:, g * PASS:(g + 1) * PASS],
@@ -153,7 +163,7 @@ def tile_stereo_softmax_code_mix_s9_kernel(tc, left, right_words, right_scales, 
 
         def correlate(i, g):
             words, scales = left_q[i]
-            bank = acc_bank("corr")
+            bank = next_bank([P, PASS], F32, "corr")
             for c in range(K_PASSES):
                 nc.tensor.matmul_mx(
                     out=bank[:],
@@ -185,7 +195,7 @@ def tile_stereo_softmax_code_mix_s9_kernel(tc, left, right_words, right_scales, 
             nc.vector.reciprocal(out=inv_mass[:, lo:hi], in_=means[:, lo:hi])
 
         def mix(i):
-            bank = acc_bank("mix")
+            bank = next_bank([P, PASS], F32, "mix")
             for g in range(GROUPS):
                 h, c = divmod(g, 2)
                 words, scales = w_q[i, h]
@@ -200,9 +210,12 @@ def tile_stereo_softmax_code_mix_s9_kernel(tc, left, right_words, right_scales, 
             mixes[i] = bank
 
         def finish(i):
-            result = work.tile([P, D], F32, tag="result", name="result")
-            nc.scalar.activation(out=result[:], in_=mixes[i][:], func=ACT.Copy, scale=inv_mass[:, i:i + 1])
-            nc.sync.dma_start(out=out[i * P:(i + 1) * P, :], in_=result[:])
+            width = D // 2 if i == TILES - 1 else D
+            for lo in range(0, D, width):
+                result = work.tile([P, width], F32, tag="result", name="result")
+                nc.scalar.activation(out=result[:], in_=mixes[i][:, lo:lo + width], func=ACT.Copy,
+                                     scale=inv_mass[:, i:i + 1])
+                nc.sync.dma_start(out=out[i * P:(i + 1) * P, lo:lo + width], in_=result[:])
 
         turn_left(0)
         copy_turned(("left", 0), True)
@@ -215,6 +228,8 @@ def tile_stereo_softmax_code_mix_s9_kernel(tc, left, right_words, right_scales, 
         turned_n = quantised = 0
         for i in range(TILES):
             if 1 <= i < last:
+                if 9 <= i + 2 < TILES:
+                    sort_left(i + 2)
                 quantise_left(i + 1)
             to_quantise = halves[quantised:turned_n]
             quantised = turned_n
@@ -238,6 +253,8 @@ def tile_stereo_softmax_code_mix_s9_kernel(tc, left, right_words, right_scales, 
                 interleave_codes(0)
                 quantise_codes(0)
                 quantise_left(1)
+                if 9 <= 2:
+                    sort_left(2)
                 weigh(*halves[0])
             elif i < GROUPS:
                 interleave_codes(i)
@@ -257,7 +274,7 @@ def tile_stereo_softmax_code_mix_s9_kernel(tc, left, right_words, right_scales, 
             if i >= TURN_START:
                 count = 2 if i + 2 < TILES else 4
                 for n, half in enumerate(halves[turned_n:turned_n + count]):
-                    turn_w(*half, n == 3)
+                    turn_w(*half)
                     copy_turned(("w",) + half, n != 0 or i < 6)
                 turned_n = turned_n + count
 

@@ -23,7 +23,8 @@ TILES = M // P
 K_PASSES = K // PASS
 GROUPS = N // PASS
 HALVES = GROUPS // 2
-MIX_LAG = 4
+HALF = N // HALVES
+MIX_LAG = 5
 TURN_START = 3
 
 
@@ -42,18 +43,15 @@ def tile_stereo_softmax_code_mix_s9_kernel(tc, left, right_words, right_scales, 
             return psum.tile(shape, dtype, tag="bank%d" % (len(handed_out) % 8), name=name)
 
         r_scales = keep.tile([P, K_PASSES, N], U8, align_bytes=256)
-        zeros = keep.tile([P, PASS], BF16)
+        zeros = keep.tile([P, P], BF16)
         vis_row = keep.tile([P, N], BF16)
-        nc.vector.memset(zeros[:].bitcast(I32), 0)
         nc.vector.memset(r_scales[:].bitcast(I32), 0)
+        nc.vector.memset(zeros[:].bitcast(I32), 0)
         nc.vector.memset(vis_row[:].bitcast(I32), 0)
         ident = keep.tile([P, P], F32)
         make_identity(nc, ident[:])
         ones = keep.tile([P, P], BF16)
         nc.scalar.activation(out=ones[:], in_=zeros[:, :P], func=ACT.Exp)
-        warm = next_bank([P, PASS], F32, "warm")
-        for n in range(4):
-            nc.tensor.matmul(warm[:], lhsT=zeros[:, :P], rhs=zeros[:], start=True, stop=True)
 
         left_raw = [keep.tile([P, K], BF16, name="left_raw%d" % i) for i in range(TILES)]
         r_words = [keep.tile([P, K_PASSES, 2 * PASS], U8, align_bytes=256, name="r_words%d" % g) for g in range(GROUPS)]
@@ -70,15 +68,21 @@ def tile_stereo_softmax_code_mix_s9_kernel(tc, left, right_words, right_scales, 
             src = codes[g * PASS:(g + 1) * PASS, :].rearrange("(p t) d -> p t d", t=4)
             nc.sync.dma_start(out=codes_raw[g][:], in_=src)
 
+        def load_scales():
+            for q in range(4):
+                src = right_scales[:, 4 * q:4 * q + 4, :].rearrange("c r n -> r c n")
+                nc.sync.dma_start(out=r_scales[32 * q:32 * q + 4, :, :].bitcast(I32), in_=src.bitcast(I32))
+
+        def load_vis():
+            nc.sync.dma_start(out=vis_row[0:1, :], in_=vis.rearrange("(o n) -> o n", o=1))
+
         load_left(0)
-        for r in range(4):
-            src = right_scales[:, 4 * r:4 * r + 4, :].rearrange("c q n -> q c n")
-            nc.sync.dma_start(out=r_scales[32 * r:32 * r + 4, :, :].bitcast(I32), in_=src.bitcast(I32))
-        nc.sync.dma_start(out=vis_row[0:1, :], in_=vis.rearrange("(o n) -> o n", o=1))
         load_right(0)
-        load_right(1)
-        load_codes(0)
+        load_scales()
+        load_vis()
         load_left(1)
+        load_codes(0)
+        load_right(1)
         load_right(2)
         load_right(3)
         for g in range(1, GROUPS):
@@ -115,20 +119,27 @@ def tile_stereo_softmax_code_mix_s9_kernel(tc, left, right_words, right_scales, 
 
         def turn_w(i, h):
             bank = next_bank([P, 4, P], F32, "w_bank")
-            words = w_tiles[i, h][:].bitcast(F32)
+            words = w_tiles[i][:].bitcast(F32)
             for s in range(4):
-                nc.tensor.transpose(bank[:, s, :], words[:, P * s:P * (s + 1)], ident[:])
+                nc.tensor.transpose(bank[:, s, :], words[:, P * (4 * h + s):P * (4 * h + s + 1)], ident[:])
             banks["w", i, h] = bank
 
-        def copy_turned(key, on_scalar):
-            dst = work.tile([P, 2 * PASS], BF16, tag="turned", bufs=8, align_bytes=256, name="turned")
-            src = banks[key][:].rearrange("p (c u) m -> p c m u", u=2)
-            dst_words = dst[:].bitcast(F32).rearrange("p (c m u) -> p c m u", c=2, u=2)
+        def copy_turned(dst, bank, on_scalar):
+            src = bank[:].rearrange("p (c u) m -> p c m u", u=2)
+            dst_words = dst.bitcast(F32).rearrange("p (c m u) -> p c m u", c=2, u=2)
             if on_scalar:
                 nc.scalar.copy(out=dst_words, in_=src)
             else:
                 nc.vector.tensor_copy(out=dst_words, in_=src)
-            turned[key] = dst
+
+        def copy_left(i, on_scalar=True):
+            turned["left", i] = work.tile([P, K], BF16, tag="left_turned", bufs=3, align_bytes=256, name="left_turned")
+            copy_turned(turned["left", i][:], banks["left", i], on_scalar)
+
+        def copy_w(i, h, on_scalar):
+            if h == 0:
+                turned["w", i] = work.tile([P, N], BF16, tag="w_turned", bufs=4, align_bytes=256, name="w_turned")
+            copy_turned(turned["w", i][:, h * HALF:(h + 1) * HALF], banks["w", i, h], on_scalar)
 
         def quantise(src, fmt, tag, bufs):
             width = src.shape[1] // 4
@@ -140,8 +151,8 @@ def tile_stereo_softmax_code_mix_s9_kernel(tc, left, right_words, right_scales, 
         def quantise_left(i):
             left_q[i] = quantise(turned["left", i][:], E4M3X4, "left", 3)
 
-        def quantise_w(i, h):
-            w_q[i, h] = quantise(turned["w", i, h][:], E5M2X4, "w", 12)
+        def quantise_w(i):
+            w_q[i] = quantise(turned["w", i][:], E5M2X4, "w", 6)
 
         def interleave_codes(g):
             dst = work.tile([P, D, 4], BF16, tag="codes_il", bufs=2, align_bytes=256, name="codes_il")
@@ -172,18 +183,18 @@ def tile_stereo_softmax_code_mix_s9_kernel(tc, left, right_words, right_scales, 
                     rhs=r_words[g][:, c, :].bitcast(E2M1X4),
                     rhs_scale=r_scales[:, c, g * PASS:(g + 1) * PASS],
                     start=(c == 0), stop=(c == K_PASSES - 1))
-            h, c = divmod(g, 2)
-            if c == 0:
-                e_tiles[i, h] = work.tile([P, 2 * PASS], F32, tag="e", bufs=10, name="e")
-            dst = e_tiles[i, h][:, c * PASS:(c + 1) * PASS].rearrange("m (u p e) -> m u p e", u=2, e=2)
+            if g == 0:
+                e_tiles[i] = work.tile([P, N], F32, tag="e", bufs=5, name="e")
+            dst = e_tiles[i][:, g * PASS:(g + 1) * PASS].rearrange("m (u p e) -> m u p e", u=2, e=2)
             nc.scalar.activation(out=dst, in_=bank[:].rearrange("m (p u e) -> m u p e", u=2, e=2), func=ACT.Exp,
                                  accum_out=sums[:, i, g:g + 1])
 
-        def weigh(i, h):
-            w = work.tile([P, 2 * PASS], BF16, tag="w", bufs=8, name="w")
-            nc.vector.tensor_tensor(out=w[:], in0=e_tiles[i, h][:],
-                                    in1=vis_all[:, 2 * PASS * h:2 * PASS * (h + 1)], op=ALU.mult)
-            w_tiles[i, h] = w
+        def weigh(first, end):
+            for i in range(first // 2, (end + 1) // 2):
+                cols = slice(max(first - 2 * i, 0) * HALF, min(end - 2 * i, 2) * HALF)
+                if cols.start == 0:
+                    w_tiles[i] = work.tile([P, N], BF16, tag="w", bufs=5, name="w")
+                nc.vector.tensor_tensor(out=w_tiles[i][:, cols], in0=e_tiles[i][:, cols], in1=vis_all[:, cols], op=ALU.mult)
 
         def add_up(lo, hi):
             nc.vector.tensor_reduce(out=totals[:, lo:hi], in_=sums[:, lo:hi, :], axis=mybir.AxisListType.X, op=ALU.add)
@@ -197,13 +208,12 @@ def tile_stereo_softmax_code_mix_s9_kernel(tc, left, right_words, right_scales, 
         def mix(i):
             bank = next_bank([P, PASS], F32, "mix")
             for g in range(GROUPS):
-                h, c = divmod(g, 2)
-                words, scales = w_q[i, h]
+                words, scales = w_q[i]
                 c_words, c_scales = codes_q[g]
                 nc.tensor.matmul_mx(
                     out=bank[:],
-                    lhsT=words[:, c * P:(c + 1) * P].bitcast(E5M2X4),
-                    lhsT_scale=scales[:, c * P:(c + 1) * P],
+                    lhsT=words[:, g * P:(g + 1) * P].bitcast(E5M2X4),
+                    lhsT_scale=scales[:, g * P:(g + 1) * P],
                     rhs=c_words[:].bitcast(E4M3X4),
                     rhs_scale=c_scales[:],
                     start=(g == 0), stop=(g == GROUPS - 1))
@@ -218,81 +228,77 @@ def tile_stereo_softmax_code_mix_s9_kernel(tc, left, right_words, right_scales, 
                 nc.sync.dma_start(out=out[i * P:(i + 1) * P, lo:lo + width], in_=result[:])
 
         turn_left(0)
-        copy_turned(("left", 0), True)
+        copy_left(0)
         quantise_left(0)
         for h in range(HALVES):
             spread_vis(h)
+        turn_left(1)
+        copy_left(1)
 
         last = TILES - 1
-        halves = [(i, h) for i in range(TILES) for h in range(HALVES)]
-        turned_n = quantised = 0
+        weighed = turned_n = quantised = 0
         for i in range(TILES):
-            if 1 <= i < last:
-                if 9 <= i + 2 < TILES:
-                    sort_left(i + 2)
-                quantise_left(i + 1)
-            to_quantise = halves[quantised:turned_n]
-            quantised = turned_n
             batch = (i - 3, i) if i > 0 and i % 3 == 0 else None
             if batch:
                 add_up(*batch)
-            for half in to_quantise[:1]:
-                quantise_w(*half)
+            if 1 <= i < last:
+                quantise_left(i + 1)
             if batch:
                 average(*batch)
-            for half in to_quantise[1:]:
-                quantise_w(*half)
-            if batch:
-                invert(*batch)
-            correlate(i, 0)
-            correlate(i, 1)
-            if i == 0:
-                turn_left(1)
-                copy_turned(("left", 1), True)
+            if i >= 1 and 5 <= i + 2 < TILES:
+                sort_left(i + 2)
+            if i == last:
+                for j in range(quantised, turned_n):
+                    quantise_w(j)
+                quantised = turned_n
+            for g in range(GROUPS):
+                correlate(i, g)
             if i == 0:
                 interleave_codes(0)
                 quantise_codes(0)
                 quantise_left(1)
-                if 9 <= 2:
-                    sort_left(2)
-                weigh(*halves[0])
-            elif i < GROUPS:
-                interleave_codes(i)
-                weigh(*halves[i])
+            end = i + 1 if i + 1 < GROUPS else min(3 * i - 4, HALVES * TILES)
+            middle = min(weighed + 2 - weighed % 2, end)
+            weigh(weighed, middle)
+            if 1 <= i < GROUPS:
                 quantise_codes(i)
-            correlate(i, 2)
-            correlate(i, 3)
-            if i >= GROUPS:
-                for half in halves[3 * i - 8:3 * i - 5]:
-                    weigh(*half)
+            for j in range(quantised, turned_n):
+                quantise_w(j)
+            quantised = turned_n
+            if i + 1 < GROUPS:
+                interleave_codes(i + 1)
+            if middle < end:
+                weigh(middle, end)
+            weighed = end
+            if batch:
+                invert(*batch)
             if i >= MIX_LAG:
                 mix(i - MIX_LAG)
                 finish(i - MIX_LAG)
             if i + 2 < TILES:
                 turn_left(i + 2)
-                copy_turned(("left", i + 2), True)
+                copy_left(i + 2, True)
             if i >= TURN_START:
-                count = 2 if i + 2 < TILES else 4
-                for n, half in enumerate(halves[turned_n:turned_n + count]):
-                    turn_w(*half)
-                    copy_turned(("w",) + half, n != 0 or i < 6)
+                count = 1 if i + 2 < TILES else 2
+                for n, j in enumerate(range(turned_n, turned_n + count)):
+                    for h in range(HALVES):
+                        turn_w(j, h)
+                        copy_w(j, h, i != 6 or h == 0)
                 turned_n = turned_n + count
 
         rest = (last // 3 * 3, TILES)
         add_up(*rest)
-        for n, half in enumerate(halves[quantised:turned_n]):
-            quantise_w(*half)
-            if n == 0:
-                average(*rest)
-            if n == 1:
-                invert(*rest)
-        mix(TILES - MIX_LAG)
-        finish(TILES - MIX_LAG)
-        for n, half in enumerate(halves[turned_n:]):
-            turn_w(*half)
-            copy_turned(("w",) + half, n != 1)
-        for half in halves[turned_n:]:
-            quantise_w(*half)
-        for i in range(TILES - MIX_LAG + 1, TILES):
+        quantise_w(last - 2)
+        average(*rest)
+        quantise_w(last - 1)
+        invert(*rest)
+        for i in range(TILES - MIX_LAG, TILES - 3):
+            mix(i)
+            finish(i)
+        for h in range(HALVES):
+            turn_w(last, h)
+            copy_w(last, h, h == 0)
+        quantise_w(last)
+        for i in range(TILES - 3, TILES):
             mix(i)
             finish(i)

from contextlib import ExitStack

import concourse.mybir as mybir
from concourse.masks import make_identity

M, K, N, D = 1024, 1024, 2048, 512
FLOPS = 2 * M * K * N + 2 * M * N * D

F32 = mybir.dt.float32
BF16 = mybir.dt.bfloat16
I32 = mybir.dt.int32
U32 = mybir.dt.uint32
U8 = mybir.dt.uint8
E4M3X4 = mybir.dt.float8_e4m3fn_x4
E5M2X4 = mybir.dt.float8_e5m2_x4
E2M1X4 = mybir.dt.float4_e2m1fn_x4
ACT = mybir.ActivationFunctionType
ALU = mybir.AluOpType

P = 128
PASS = 512
TILES = M // P
K_PASSES = K // PASS
GROUPS = N // PASS
HALVES = GROUPS // 2
HALF = N // HALVES
MIX_LAG = 5
TURN_START = 3


def tile_stereo_softmax_code_mix_s9_kernel(tc, left, right_words, right_scales, vis, codes, out):
    nc = tc.nc
    with ExitStack() as ctx:
        keep = ctx.enter_context(tc.tile_pool(name="keep", bufs=1))
        work = ctx.enter_context(tc.tile_pool(name="work", bufs=4))
        psum = ctx.enter_context(tc.psum_pool(name="psum", bufs=1))
        ctx.enter_context(tc.manual_schedule())

        handed_out = []

        def next_bank(shape, dtype, name):
            handed_out.append(name)
            return psum.tile(shape, dtype, tag="bank%d" % (len(handed_out) % 8), name=name)

        r_scales = keep.tile([P, K_PASSES, N], U8, align_bytes=256)
        zeros = keep.tile([P, P], BF16)
        vis_row = keep.tile([P, N], BF16)
        nc.vector.memset(r_scales[:].bitcast(I32), 0)
        nc.vector.memset(zeros[:].bitcast(I32), 0)
        nc.vector.memset(vis_row[:].bitcast(I32), 0)
        ident = keep.tile([P, P], F32)
        make_identity(nc, ident[:])
        ones = keep.tile([P, P], BF16)
        nc.scalar.activation(out=ones[:], in_=zeros[:, :P], func=ACT.Exp)

        left_raw = [keep.tile([P, K], BF16, name="left_raw%d" % i) for i in range(TILES)]
        r_words = [keep.tile([P, K_PASSES, 2 * PASS], U8, align_bytes=256, name="r_words%d" % g) for g in range(GROUPS)]
        codes_raw = [keep.tile([P, 4, D], BF16, name="codes_raw%d" % g) for g in range(GROUPS)]

        def load_left(i):
            nc.sync.dma_start(out=left_raw[i][:], in_=left[i * P:(i + 1) * P, :])

        def load_right(g):
            src = right_words[:, :, 2 * PASS * g:2 * PASS * (g + 1)].rearrange("c p n -> p c n")
            nc.sync.dma_start(out=r_words[g][:].bitcast(I32), in_=src.bitcast(I32))

        def load_codes(g):
            src = codes[g * PASS:(g + 1) * PASS, :].rearrange("(p t) d -> p t d", t=4)
            nc.sync.dma_start(out=codes_raw[g][:], in_=src)

        def load_scales():
            for q in range(4):
                src = right_scales[:, 4 * q:4 * q + 4, :].rearrange("c r n -> r c n")
                nc.sync.dma_start(out=r_scales[32 * q:32 * q + 4, :, :].bitcast(I32), in_=src.bitcast(I32))

        def load_vis():
            nc.sync.dma_start(out=vis_row[0:1, :], in_=vis.rearrange("(o n) -> o n", o=1))

        load_left(0)
        load_right(0)
        load_scales()
        load_vis()
        load_left(1)
        load_codes(0)
        load_right(1)
        load_right(2)
        load_right(3)
        for g in range(1, GROUPS):
            load_left(g + 1)
            load_codes(g)
        for i in range(GROUPS + 1, TILES):
            load_left(i)

        banks, turned, left_q, e_tiles, w_tiles, w_q, codes_il, codes_q = {}, {}, {}, {}, {}, {}, {}, {}
        mixes, left_sorted = {}, {}
        sums = keep.tile([P, TILES, GROUPS], F32, name="sums")
        totals = keep.tile([P, TILES], F32, name="totals")
        means = keep.tile([P, TILES], F32, name="means")
        inv_mass = keep.tile([P, TILES], F32, name="inv_mass")
        vis_all = keep.tile([P, N], BF16)

        def sort_left(i):
            dst = work.tile([P, K_PASSES, 2, P], F32, tag="left_sorted", bufs=3, name="left_sorted")
            src = left_raw[i][:].bitcast(F32).rearrange("m (c p u) -> m c u p", c=K_PASSES, u=2)
            nc.vector.tensor_copy(out=dst[:], in_=src)
            left_sorted[i] = dst

        def turn_left(i):
            bank = next_bank([P, 4, P], F32, "left_bank")
            words = left_raw[i][:].bitcast(F32)
            for c in range(K_PASSES):
                for u in range(2):
                    if i in left_sorted:
                        src = left_sorted[i][:, c, u, :]
                    else:
                        src = words[:, 256 * c + u:256 * (c + 1):2]
                    nc.tensor.transpose(bank[:, 2 * c + u, :], src, ident[:])
            banks["left", i] = bank

        def turn_w(i, h):
            bank = next_bank([P, 4, P], F32, "w_bank")
            words = w_tiles[i][:].bitcast(F32)
            for s in range(4):
                nc.tensor.transpose(bank[:, s, :], words[:, P * (4 * h + s):P * (4 * h + s + 1)], ident[:])
            banks["w", i, h] = bank

        def copy_turned(dst, bank, on_scalar):
            src = bank[:].rearrange("p (c u) m -> p c m u", u=2)
            dst_words = dst.bitcast(F32).rearrange("p (c m u) -> p c m u", c=2, u=2)
            if on_scalar:
                nc.scalar.copy(out=dst_words, in_=src)
            else:
                nc.vector.tensor_copy(out=dst_words, in_=src)

        def copy_left(i, on_scalar=True):
            turned["left", i] = work.tile([P, K], BF16, tag="left_turned", bufs=3, align_bytes=256, name="left_turned")
            copy_turned(turned["left", i][:], banks["left", i], on_scalar)

        def copy_w(i, h, on_scalar):
            if h == 0:
                turned["w", i] = work.tile([P, N], BF16, tag="w_turned", bufs=4, align_bytes=256, name="w_turned")
            copy_turned(turned["w", i][:, h * HALF:(h + 1) * HALF], banks["w", i, h], on_scalar)

        def quantise(src, fmt, tag, bufs):
            width = src.shape[1] // 4
            words = work.tile([P, width], U32, tag=tag + "_words", bufs=bufs, align_bytes=256, name=tag + "_words")
            scales = work.tile([P, width], U8, tag=tag + "_scales", bufs=bufs, align_bytes=256, name=tag + "_scales")
            nc.vector.quantize_mx(out=words[:].bitcast(fmt), scales=scales[:], in_=src)
            return words, scales

        def quantise_left(i):
            left_q[i] = quantise(turned["left", i][:], E4M3X4, "left", 3)

        def quantise_w(i):
            w_q[i] = quantise(turned["w", i][:], E5M2X4, "w", 6)

        def interleave_codes(g):
            dst = work.tile([P, D, 4], BF16, tag="codes_il", bufs=2, align_bytes=256, name="codes_il")
            nc.vector.tensor_copy(out=dst[:].rearrange("p (c i) t -> p c t i", i=4),
                                  in_=codes_raw[g][:].rearrange("p t (c i) -> p c t i", i=4))
            codes_il[g] = dst

        def quantise_codes(g):
            codes_q[g] = quantise(codes_il[g][:].rearrange("p d t -> p (d t)"), E4M3X4, "codes", GROUPS)

        def spread_vis(h):
            bank = next_bank([P, 2 * PASS], BF16, "vis_bank")
            for c in range(2):
                g = 2 * h + c
                nc.tensor.matmul(bank[:, c * PASS:(c + 1) * PASS], lhsT=ones[:], rhs=vis_row[:, g * PASS:(g + 1) * PASS],
                                 start=True, stop=True)
            dst = vis_all[:, 2 * PASS * h:2 * PASS * (h + 1)].rearrange("q (c u p e) -> q c u p e", c=2, u=2, e=2)
            nc.scalar.copy(out=dst, in_=bank[:].rearrange("q (c p u e) -> q c u p e", c=2, u=2, e=2))

        def correlate(i, g):
            words, scales = left_q[i]
            bank = next_bank([P, PASS], F32, "corr")
            for c in range(K_PASSES):
                nc.tensor.matmul_mx(
                    out=bank[:],
                    lhsT=words[:, c * P:(c + 1) * P].bitcast(E4M3X4),
                    lhsT_scale=scales[:, c * P:(c + 1) * P],
                    rhs=r_words[g][:, c, :].bitcast(E2M1X4),
                    rhs_scale=r_scales[:, c, g * PASS:(g + 1) * PASS],
                    start=(c == 0), stop=(c == K_PASSES - 1))
            if g == 0:
                e_tiles[i] = work.tile([P, N], F32, tag="e", bufs=5, name="e")
            dst = e_tiles[i][:, g * PASS:(g + 1) * PASS].rearrange("m (u p e) -> m u p e", u=2, e=2)
            nc.scalar.activation(out=dst, in_=bank[:].rearrange("m (p u e) -> m u p e", u=2, e=2), func=ACT.Exp,
                                 accum_out=sums[:, i, g:g + 1])

        def weigh(first, end):
            for i in range(first // 2, (end + 1) // 2):
                cols = slice(max(first - 2 * i, 0) * HALF, min(end - 2 * i, 2) * HALF)
                if cols.start == 0:
                    w_tiles[i] = work.tile([P, N], BF16, tag="w", bufs=5, name="w")
                nc.vector.tensor_tensor(out=w_tiles[i][:, cols], in0=e_tiles[i][:, cols], in1=vis_all[:, cols], op=ALU.mult)

        def add_up(lo, hi):
            nc.vector.tensor_reduce(out=totals[:, lo:hi], in_=sums[:, lo:hi, :], axis=mybir.AxisListType.X, op=ALU.add)

        def average(lo, hi):
            nc.vector.tensor_scalar(out=means[:, lo:hi], in0=totals[:, lo:hi], scalar1=1.0 / N, scalar2=None, op0=ALU.mult)

        def invert(lo, hi):
            nc.vector.reciprocal(out=inv_mass[:, lo:hi], in_=means[:, lo:hi])

        def mix(i):
            bank = next_bank([P, PASS], F32, "mix")
            for g in range(GROUPS):
                words, scales = w_q[i]
                c_words, c_scales = codes_q[g]
                nc.tensor.matmul_mx(
                    out=bank[:],
                    lhsT=words[:, g * P:(g + 1) * P].bitcast(E5M2X4),
                    lhsT_scale=scales[:, g * P:(g + 1) * P],
                    rhs=c_words[:].bitcast(E4M3X4),
                    rhs_scale=c_scales[:],
                    start=(g == 0), stop=(g == GROUPS - 1))
            mixes[i] = bank

        def finish(i):
            width = D // 2 if i == TILES - 1 else D
            for lo in range(0, D, width):
                result = work.tile([P, width], F32, tag="result", name="result")
                nc.scalar.activation(out=result[:], in_=mixes[i][:, lo:lo + width], func=ACT.Copy,
                                     scale=inv_mass[:, i:i + 1])
                nc.sync.dma_start(out=out[i * P:(i + 1) * P, lo:lo + width], in_=result[:])

        turn_left(0)
        copy_left(0)
        quantise_left(0)
        for h in range(HALVES):
            spread_vis(h)
        turn_left(1)
        copy_left(1)

        last = TILES - 1
        weighed = turned_n = quantised = 0
        for i in range(TILES):
            batch = (i - 3, i) if i > 0 and i % 3 == 0 else None
            if batch:
                add_up(*batch)
            if 1 <= i < last:
                quantise_left(i + 1)
            if batch:
                average(*batch)
            if i >= 1 and 5 <= i + 2 < TILES:
                sort_left(i + 2)
            if i == last:
                for j in range(quantised, turned_n):
                    quantise_w(j)
                quantised = turned_n
            for g in range(GROUPS):
                correlate(i, g)
            if i == 0:
                interleave_codes(0)
                quantise_codes(0)
                quantise_left(1)
            end = i + 1 if i + 1 < GROUPS else min(3 * i - 4, HALVES * TILES)
            middle = min(weighed + 2 - weighed % 2, end)
            weigh(weighed, middle)
            if 1 <= i < GROUPS:
                quantise_codes(i)
            for j in range(quantised, turned_n):
                quantise_w(j)
            quantised = turned_n
            if i + 1 < GROUPS:
                interleave_codes(i + 1)
            if middle < end:
                weigh(middle, end)
            weighed = end
            if batch:
                invert(*batch)
            if i >= MIX_LAG:
                mix(i - MIX_LAG)
                finish(i - MIX_LAG)
            if i + 2 < TILES:
                turn_left(i + 2)
                copy_left(i + 2, True)
            if i >= TURN_START:
                count = 1 if i + 2 < TILES else 2
                for n, j in enumerate(range(turned_n, turned_n + count)):
                    for h in range(HALVES):
                        turn_w(j, h)
                        copy_w(j, h, i != 6 or h == 0)
                turned_n = turned_n + count

        rest = (last // 3 * 3, TILES)
        add_up(*rest)
        quantise_w(last - 2)
        average(*rest)
        quantise_w(last - 1)
        invert(*rest)
        for i in range(TILES - MIX_LAG, TILES - 3):
            mix(i)
            finish(i)
        for h in range(HALVES):
            turn_w(last, h)
            copy_w(last, h, h == 0)
        quantise_w(last)
        for i in range(TILES - 3, TILES):
            mix(i)
            finish(i)
